import numpy as np
import ml_dtypes


def mxq(x, axis, fmt="e4m3"):
    dtype, down = {"e4m3": (ml_dtypes.float8_e4m3fn, 7), "e5m2": (ml_dtypes.float8_e5m2, 14)}[fmt]
    v = np.moveaxis(np.asarray(x, np.float32).astype(ml_dtypes.bfloat16).astype(np.float64), axis, -1)
    blocks = v.reshape(v.shape[:-1] + (-1, 32))
    amax = np.abs(blocks).max(-1, keepdims=True)
    byte = np.maximum(np.where(amax > 0, np.frexp(amax)[1] - 1 + 127, 0) - down, 1)
    scale = np.exp2(byte - 127.0)
    codes = (blocks / scale).astype(np.float32).astype(dtype).astype(np.float64)
    return np.moveaxis((codes * scale).reshape(v.shape), -1, axis)


WIDE = False


def mx_kscale(k):
    if not WIDE:
        return np.ones(k)
    levels = np.array([10, -10, 5, -5, 0])
    if k % 512:
        return np.exp2(np.random.permutation(np.resize(levels, k // 32))).repeat(32)
    a = np.empty((k // 512, 16))
    for p in range(k // 512):
        a[p, :8] = np.random.permutation(np.resize(levels, 8))
        for g in range(8):
            far = levels[np.abs(levels - a[p, g]) >= 10]
            a[p, g + 8] = far[np.random.randint(len(far))]
    return np.exp2(a.ravel()).repeat(32)


def f64(x):
    return np.asarray(x).astype(np.float64)


def striped(idx):
    return np.tile(np.asarray(idx).reshape(-1, 16).T, (8, 1)).astype(np.uint16)


def unstriped(offs):
    return offs[:16].T.reshape(-1).astype(np.int64)


E2M1 = np.array([0.0, 0.5, 1.0, 1.5, 2.0, 3.0, 4.0, 6.0, -0.0, -0.5, -1.0, -1.5, -2.0, -3.0, -4.0, -6.0])


def pack_weight(w, fmt):
    k, n = w.shape
    w = f64(np.asarray(w, np.float32).astype(ml_dtypes.bfloat16)).reshape(k // 32, 32, n)
    amax = np.abs(w).max(1)
    if fmt == "e4m3":
        byte = np.frexp(amax)[1] - 1 + 127 - 7
    else:
        mant, ex = np.frexp(amax / 6.0)
        byte = np.where(mant > 0.5, ex, ex - 1) + 127
    byte = np.clip(np.where(amax > 0, byte, 1), 1, 254)
    scaled = (w * np.exp2(127.0 - byte)[:, None, :]).reshape(k, n).astype(np.float32)
    by_word = np.ascontiguousarray(scaled.reshape(k // 512, 128, 4, n).transpose(0, 1, 3, 2))
    if fmt == "e4m3":
        words = by_word.astype(ml_dtypes.float8_e4m3fn).view(np.uint8)
    else:
        c = by_word.astype(ml_dtypes.float4_e2m1fn).view(np.uint8) & 0xF
        words = (c[..., 0::2] | (c[..., 1::2] << 4)).reshape(k // 512, 128, 2 * n)
    return np.ascontiguousarray(words), np.ascontiguousarray(byte.astype(np.uint8).reshape(k // 512, 16, n))


def unpack_weight(words, scales, fmt):
    g, _, n = scales.shape
    words = np.ascontiguousarray(words).reshape(g, 128, n, -1)
    if fmt == "e4m3":
        vals = words.view(ml_dtypes.float8_e4m3fn).astype(np.float64)
    else:
        nib = np.empty((g, 128, n, 4), np.uint8)
        nib[..., 0::2] = words & 0xF
        nib[..., 1::2] = words >> 4
        vals = E2M1[nib]
    vals = vals * np.repeat(np.exp2(scales.astype(np.float64) - 127.0), 8, axis=1)[..., None]
    return vals.transpose(0, 1, 3, 2).reshape(g * 512, n)


D, K, R, T, I, Q, G = 512, 512, 512, 2048, 512, 128, 64


def setup_inputs():
    n = np.random.standard_normal
    idx = np.random.permutation(T)[:I]
    fd = mx_kscale(D)
    fk = mx_kscale(K)
    fi = mx_kscale(I)
    keysp = pack_weight(n((D, T)) / fd[:, None], "e2m1")
    tabp = pack_weight(n((K, T)) / fk[:, None], "e2m1")
    return {
        "query": (n((D, Q)) * 0.6 / np.sqrt(D) * fd[:, None]).astype(np.float32),
        "keys_words": keysp[0],
        "keys_scales": keysp[1],
        "sharp": (np.random.uniform(1.0, 3.0, (Q, 1))).astype(np.float32),
        "tab_words": tabp[0],
        "tab_scales": tabp[1],
        "w1": (n((K, R)) * 1 / np.sqrt(K) * fk[:, None]).astype(np.float32),
        "gain": (np.random.uniform(0.5, 2.0, (R, 1))).astype(np.float32),
        "os": (np.random.uniform(4.0, 16.0, (1, I)) * fi).astype(np.float32),
        "vs": (np.random.uniform(0.5, 2.0, (1, I)) / fi).astype(np.float32),
        "offs": striped(idx),
    }


def reference(query, keys_words, keys_scales, sharp, tab_words, tab_scales, w1, gain, os, vs, offs):
    idx = unstriped(offs)
    keysu = unpack_weight(keys_words, keys_scales, "e2m1")
    tabu = unpack_weight(tab_words, tab_scales, "e2m1")
    queryq = mxq(f64(query), 0, "e4m3")
    keysidxg = keysu[:, idx]
    a = queryq.T @ keysidxg
    p = np.exp(a)
    s = p.reshape(Q, G, I // G).sum(axis=2)
    ms = a.reshape(Q, G, I // G).mean(axis=2) * f64(sharp)
    pg = np.exp(ms - np.max(ms, axis=1, keepdims=True))
    z = np.sum(pg, axis=1, keepdims=True)
    sh = pg / z / s
    rr = np.repeat(sh, I // G, axis=1)
    w = p * rr
    w1q = mxq(f64(w1), 0, "e4m3")
    tabidxg = tabu[:, idx]
    zh = w1q.T @ tabidxg
    ht = np.tanh(zh)
    hv = ht * f64(gain)
    wo1 = w * f64(os)
    wt1 = wo1.T
    hw = hv * f64(vs)
    ht1 = hw.T
    wt1q = mxq(wt1, 0, "e4m3")
    ht1q = mxq(ht1, 0, "e4m3")
    o = wt1q.T @ ht1q
    return o

@@ -1,0 +1,236 @@
+from contextlib import ExitStack
+
+import concourse.mybir as mybir
+from concourse.masks import make_identity
+
+D, K, R, T, I, Q, G = 512, 512, 512, 2048, 512, 128, 64
+FLOPS = 2 * D * Q * I + 2 * K * R * I + 2 * I * Q * R
+
+F32 = mybir.dt.float32
+BF16 = mybir.dt.bfloat16
+I32 = mybir.dt.int32
+U32 = mybir.dt.uint32
+U16 = mybir.dt.uint16
+U8 = mybir.dt.uint8
+FP8X4 = mybir.dt.float8_e4m3fn_x4
+FP4X4 = mybir.dt.float4_e2m1fn_x4
+ALU = mybir.AluOpType
+ACT = mybir.ActivationFunctionType
+AX = mybir.AxisListType
+
+P = 128
+PACK = 4
+GROUP = I // G
+HALF = R // 2
+
+
+def load_scale_rows(queue, plane, scales):
+    for quad in range(4):
+        queue.dma_start(
+            out=plane[32 * quad : 32 * quad + 4, :].bitcast(I32),
+            in_=scales[0, 4 * quad : 4 * quad + 4, :].bitcast(I32),
+        )
+
+
+def interleave(nc, grouped, raw):
+    nc.scalar.copy(
+        out=grouped.rearrange("p (c n) t -> p c t n", n=4),
+        in_=raw.rearrange("p t (c n) -> p c t n", n=4),
+    )
+
+
+def quantize(nc, codes, scales, grouped):
+    nc.vector.quantize_mx(out=codes.bitcast(FP8X4), scales=scales, in_=grouped.rearrange("p c t -> p (c t)"))
+
+
+def turn_pairs(nc, bank, values, ident, grouped):
+    words = values.bitcast(F32)
+    for u in range(2):
+        nc.tensor.transpose(bank[:, u, :], words[:, u : I // 2 : 2], ident)
+    nc.scalar.copy(
+        out=grouped.rearrange("p c t -> p (c t)").bitcast(F32).rearrange("p (c u) -> p c u", u=2),
+        in_=bank.rearrange("p u c -> p c u"),
+    )
+
+
+def tile_attend_lrgained_bygroup_kernel(
+    tc, query, keys_words, keys_scales, sharp, tab_words, tab_scales, w1, gain, slot_factor, value_scale, offs, out
+):
+    nc = tc.nc
+    with ExitStack() as ctx:
+        held = ctx.enter_context(tc.tile_pool(name="held", bufs=1))
+        reuse = ctx.enter_context(tc.tile_pool(name="reuse", bufs=1))
+        psum = ctx.enter_context(tc.psum_pool(name="psum", bufs=1))
+
+        offsets = held.tile([P, I // 16], U16, name="offsets")
+        key_pool = held.tile([P, T], U16, name="key_pool")
+        key_pool_scales = held.tile([P, T], U8, name="key_pool_scales")
+        tab_pool = held.tile([P, T], U16, name="tab_pool")
+        tab_pool_scales = held.tile([P, T], U8, name="tab_pool_scales", tag="slot_b", align_bytes=64)
+        rows = held.tile([P, P], F32, name="rows")
+        ident = held.tile([P, P], F32, name="ident")
+        q_raw = held.tile([P, PACK, Q], F32, name="q_raw")
+        w_raw = [reuse.tile([P, PACK, HALF], F32, name=f"w_raw{h}", offset=4096 * h) for h in range(2)]
+        sharp_col = held.tile([Q, 1], F32, name="sharp_col")
+
+        nc.vector.memset(key_pool_scales[:].bitcast(I32), 0)
+        nc.vector.memset(tab_pool_scales[:].bitcast(I32), 0)
+        nc.gpsimd.memset(rows[:], 0.0)
+
+        w1_rows = w1.rearrange("(p t) r -> p t r", t=PACK)
+        nc.sync.dma_start(offsets[:], offs)
+        load_scale_rows(nc.sync, key_pool_scales, keys_scales)
+        nc.sync.dma_start(out=sharp_col[:], in_=sharp)
+        nc.scalar.dma_start(out=key_pool[:].bitcast(I32), in_=keys_words[0].bitcast(I32))
+        nc.scalar.dma_start(out=tab_pool[:].bitcast(I32), in_=tab_words[0].bitcast(I32))
+        nc.scalar.dma_start(out=q_raw[:], in_=query.rearrange("(p t) q -> p t q", t=PACK))
+        nc.sync.dma_start(out=w_raw[0][:], in_=w1_rows[:, :, 0:HALF])
+        load_scale_rows(nc.sync, tab_pool_scales, tab_scales)
+        nc.sync.dma_start(out=w_raw[1][:], in_=w1_rows[:, :, HALF:R])
+        nc.gpsimd.dma_start(out=rows[0:4, :], in_=slot_factor.rearrange("o (j n) -> (o j) n", j=4))
+        nc.gpsimd.dma_start(out=rows[4:8, :], in_=value_scale.rearrange("o (j n) -> (o j) n", j=4))
+        nc.gpsimd.dma_start(out=rows[8:12, :], in_=gain.rearrange("(j n) o -> j (n o)", j=4))
+        make_identity(nc, ident[:])
+
+        warm = held.tile([P, 1], F32, name="warm")
+        warm_in = held.tile([P, 1], F32, name="warm_in")
+        nc.vector.memset(warm_in[:], 0.0)
+        nc.scalar.activation(out=warm[:], in_=warm_in[:], func=ACT.Tanh)
+
+        key_scales = held.tile([P, I], U8, name="key_scales", align_bytes=64)
+        key_words = held.tile([P, I], U16, name="key_words", align_bytes=64)
+        tab_g_words = held.tile([P, I], U16, name="tab_g_words", align_bytes=64)
+        nc.vector.tensor_copy(key_words[:], key_pool[:].indirect(offsets[:]))
+        nc.vector.tensor_copy(tab_g_words[:], tab_pool[:].indirect(offsets[:]))
+        nc.vector.tensor_copy(key_scales[:], key_pool_scales[:].indirect(offsets[:]))
+
+        q_grouped = held.tile([P, Q, PACK], BF16, name="q_grouped", tag="slot_d", align_bytes=64)
+        q_codes = held.tile([P, Q], U32, name="q_codes", align_bytes=64)
+        q_scales = held.tile([P, Q], U8, name="q_scales", align_bytes=64)
+        interleave(nc, q_grouped[:], q_raw[:])
+        quantize(nc, q_codes[:], q_scales[:], q_grouped[:])
+
+        scores = psum.tile([Q, I], F32, name="scores", tag="scores")
+        nc.tensor.matmul_mx(
+            out=scores[:],
+            lhsT=q_codes[:].bitcast(FP8X4),
+            lhsT_scale=q_scales[:],
+            rhs=key_words[:].bitcast(FP4X4),
+            rhs_scale=key_scales[:],
+            start=True,
+            stop=True,
+        )
+
+        w_grouped = [
+            held.tile([P, HALF, PACK], BF16, name=f"w_grouped{h}", tag=f"w_grouped{h}", align_bytes=64) for h in range(2)
+        ]
+        w_scales = [held.tile([P, HALF], U8, name=f"w_scales{h}", align_bytes=64) for h in range(2)]
+        interleave(nc, w_grouped[0][:], w_raw[0][:])
+
+        p = reuse.tile([Q, I], F32, name="p", offset=0)
+        nc.scalar.activation(out=p[:], in_=scores[:], func=ACT.Exp)
+
+        cols_bank = psum.tile([P, 2, P], F32, name="cols_bank", tag="turn0")
+        nc.tensor.transpose(cols_bank[:, 0, :], rows[:], ident[:])
+        cols = reuse.tile([P, 16], F32, name="cols", offset=2048)
+        nc.scalar.copy(out=cols[:], in_=cols_bank[:, 0, 0:16])
+        os_row = psum.tile([P, I], F32, name="os_row")
+        vs_row = psum.tile([P, I], F32, name="vs_row")
+        for j in range(4):
+            nc.tensor.transpose(os_row[:, j * P : (j + 1) * P], cols[:, j : j + 1].to_broadcast([P, P]), ident[:])
+        for j in range(4):
+            nc.tensor.transpose(vs_row[:, j * P : (j + 1) * P], cols[:, 4 + j : 5 + j].to_broadcast([P, P]), ident[:])
+
+        tab_g_scales = held.tile([P, I], U8, name="tab_g_scales", tag="slot_d", align_bytes=64)
+        nc.vector.tensor_copy(tab_g_scales[:], tab_pool_scales[:].indirect(offsets[:]))
+        w_codes = [
+            held.tile([P, HALF], U32, name="w_codes0", tag="slot_b", align_bytes=64),
+            held.tile([P, HALF], U32, name="w_codes1", align_bytes=64),
+        ]
+        quantize(nc, w_codes[0][:], w_scales[0][:], w_grouped[0][:])
+
+        interleave(nc, w_grouped[1][:], w_raw[1][:])
+
+        neg_sharp = held.tile([Q, 1], F32, name="neg_sharp")
+        nc.vector.tensor_scalar(neg_sharp[:], sharp_col[:], -1.0 / GROUP, None, ALU.mult)
+        score_sums = held.tile([Q, G], F32, name="score_sums", tag="w_grouped0", align_bytes=64)
+        nc.vector.tensor_reduce(score_sums[:], scores[:].rearrange("q (g j) -> q g j", j=GROUP), AX.X, ALU.add)
+        neg_ms = held.tile([Q, G], F32, name="neg_ms")
+        neg_max = held.tile([Q, 1], F32, name="neg_max")
+        nc.vector.tensor_scalar(neg_ms[:], score_sums[:], neg_sharp[:], None, ALU.mult, ALU.min, accum_out=neg_max[:])
+        s = held.tile([Q, G], F32, name="s", tag="w_grouped0", align_bytes=64)
+        nc.vector.tensor_reduce(s[:], p[:].rearrange("q (g j) -> q g j", j=GROUP), AX.X, ALU.add)
+        pg = reuse.tile([Q, G], F32, name="pg", offset=6144)
+        z = held.tile([Q, 1], F32, name="z")
+        nc.scalar.activation(out=pg[:], in_=neg_ms[:], func=ACT.Exp, bias=neg_max[:], scale=-1.0, accum_out=z[:])
+        inv_s = held.tile([Q, G], F32, name="inv_s")
+        nc.vector.reciprocal(inv_s[:], s[:])
+        quantize(nc, w_codes[1][:], w_scales[1][:], w_grouped[1][:])
+        p_os = held.tile([Q, I], F32, name="p_os")
+        nc.vector.tensor_tensor(p_os[:], p[:], os_row[:], ALU.mult)
+        inv_z = held.tile([Q, 1], F32, name="inv_z")
+        nc.vector.reciprocal(inv_z[:], z[:])
+
+        pieces = [(0, 2 * P, "scores"), (2 * P, P, "zh0"), (3 * P, P, "zh1")]
+        h_grouped = [held.tile([P, n, PACK], BF16, name=f"h_grouped{r0}", align_bytes=64) for r0, n, bank_tag in pieces]
+        h_codes = [held.tile([P, n], U32, name=f"h_codes{r0}", align_bytes=64) for r0, n, bank_tag in pieces]
+        h_scales = [held.tile([P, n], U8, name=f"h_scales{r0}", align_bytes=64) for r0, n, bank_tag in pieces]
+
+        def hidden(c):
+            h, cs = c // 2, slice((c % 2) * P, (c % 2 + 1) * P)
+            zh = psum.tile([P, I], F32, name=f"zh{c}", tag=f"zh{c % 2}")
+            nc.tensor.matmul_mx(
+                out=zh[:],
+                lhsT=w_codes[h][:, cs].bitcast(FP8X4),
+                lhsT_scale=w_scales[h][:, cs],
+                rhs=tab_g_words[:].bitcast(FP4X4),
+                rhs_scale=tab_g_scales[:],
+                start=True,
+                stop=True,
+            )
+            ht = reuse.tile([P, I], F32, name=f"ht{c}", offset=4096 if c == 0 else 6144 + 2048 * c)
+            nc.scalar.activation(out=ht[:], in_=zh[:], func=ACT.Tanh)
+            hw = held.tile([P, I], BF16, name=f"hw{c}")
+            nc.vector.scalar_tensor_tensor(hw[:], ht[:], cols[:, 8 + c : 9 + c], vs_row[:], ALU.mult, ALU.mult)
+            bank = psum.tile([P, 2, P], F32, name=f"h_bank{c}", tag=f"turn{c % 2}")
+            turn_pairs(nc, bank[:], hw[:], ident[:], h_grouped[0][:, cs, :] if c < 2 else h_grouped[c - 1][:])
+
+        hidden(0)
+        sh = held.tile([Q, G], F32, name="sh")
+        nc.vector.scalar_tensor_tensor(sh[:], pg[:], inv_z[:], inv_s[:], ALU.mult, ALU.mult)
+        hidden(1)
+        wo = held.tile([Q, I], BF16, name="wo")
+        nc.vector.tensor_tensor(
+            wo[:].rearrange("q (g j) -> q g j", j=GROUP),
+            p_os[:].rearrange("q (g j) -> q g j", j=GROUP),
+            sh[:].unsqueeze(2).to_broadcast([Q, G, GROUP]),
+            ALU.mult,
+        )
+        wo_grouped = held.tile([P, Q, PACK], BF16, name="wo_grouped", align_bytes=64)
+        wo_codes = held.tile([P, Q], U32, name="wo_codes", align_bytes=64)
+        wo_scales = held.tile([P, Q], U8, name="wo_scales", align_bytes=64)
+        wo_bank = psum.tile([P, 2, P], F32, name="wo_bank")
+        turn_pairs(nc, wo_bank[:], wo[:], ident[:], wo_grouped[:])
+
+        def finish(j):
+            r0, n, bank_tag = pieces[j]
+            quantize(nc, h_codes[j][:], h_scales[j][:], h_grouped[j][:])
+            acc = psum.tile([Q, n], F32, name=f"acc{j}", tag=bank_tag)
+            nc.tensor.matmul_mx(
+                out=acc[:],
+                lhsT=wo_codes[:].bitcast(FP8X4),
+                lhsT_scale=wo_scales[:],
+                rhs=h_codes[j][:].bitcast(FP8X4),
+                rhs_scale=h_scales[j][:],
+                start=True,
+                stop=True,
+            )
+            result = held.tile([Q, n], F32, name=f"result{j}")
+            nc.scalar.copy(out=result[:], in_=acc[:])
+            nc.sync.dma_start(out=out[:, r0 : r0 + n], in_=result[:])
+
+        hidden(2)
+        quantize(nc, wo_codes[:], wo_scales[:], wo_grouped[:])
+        hidden(3)
+        for j in range(3):
+            finish(j)

@@ -65,51 +65,54 @@ def tile_attend_lrgained_bygroup_kernel(
         offsets = held.tile([P, I // 16], U16, name="offsets")
         key_pool = held.tile([P, T], U16, name="key_pool")
         key_pool_scales = held.tile([P, T], U8, name="key_pool_scales")
-        tab_pool = held.tile([P, T], U16, name="tab_pool")
-        tab_pool_scales = held.tile([P, T], U8, name="tab_pool_scales", tag="slot_b", align_bytes=64)
-        rows = held.tile([P, P], F32, name="rows")
+        tab_pool = reuse.tile([P, T], U16, name="tab_pool", offset=12288)
+        tab_pool_scales = reuse.tile([P, T], U8, name="tab_pool_scales", offset=16384)
+        gain_rows = held.tile([P, P], F32, name="gain_rows")
         ident = held.tile([P, P], F32, name="ident")
         q_raw = held.tile([P, PACK, Q], F32, name="q_raw")
-        w_raw = [reuse.tile([P, PACK, HALF], F32, name=f"w_raw{h}", offset=4096 * h) for h in range(2)]
+        w_raw = [reuse.tile([P, PACK, HALF], F32, name=f"w_raw{h}", offset=6144 * h) for h in range(2)]
         sharp_col = held.tile([Q, 1], F32, name="sharp_col")
+        os_cols = held.tile([P, PACK], F32, name="os_cols")
+        vs_cols = held.tile([P, PACK], F32, name="vs_cols")
 
         nc.vector.memset(key_pool_scales[:].bitcast(I32), 0)
         nc.vector.memset(tab_pool_scales[:].bitcast(I32), 0)
-        nc.gpsimd.memset(rows[:], 0.0)
 
         w1_rows = w1.rearrange("(p t) r -> p t r", t=PACK)
         nc.sync.dma_start(offsets[:], offs)
+        nc.sync.dma_start(out=key_pool[:].bitcast(I32), in_=keys_words[0].bitcast(I32))
         load_scale_rows(nc.sync, key_pool_scales, keys_scales)
-        nc.sync.dma_start(out=sharp_col[:], in_=sharp)
-        nc.scalar.dma_start(out=key_pool[:].bitcast(I32), in_=keys_words[0].bitcast(I32))
-        nc.scalar.dma_start(out=tab_pool[:].bitcast(I32), in_=tab_words[0].bitcast(I32))
-        nc.scalar.dma_start(out=q_raw[:], in_=query.rearrange("(p t) q -> p t q", t=PACK))
+        nc.sync.dma_start(out=q_raw[:], in_=query.rearrange("(p t) q -> p t q", t=PACK))
         nc.sync.dma_start(out=w_raw[0][:], in_=w1_rows[:, :, 0:HALF])
         load_scale_rows(nc.sync, tab_pool_scales, tab_scales)
+        nc.sync.dma_start(out=tab_pool[:].bitcast(I32), in_=tab_words[0].bitcast(I32))
         nc.sync.dma_start(out=w_raw[1][:], in_=w1_rows[:, :, HALF:R])
-        nc.gpsimd.dma_start(out=rows[0:4, :], in_=slot_factor.rearrange("o (j n) -> (o j) n", j=4))
-        nc.gpsimd.dma_start(out=rows[4:8, :], in_=value_scale.rearrange("o (j n) -> (o j) n", j=4))
-        nc.gpsimd.dma_start(out=rows[8:12, :], in_=gain.rearrange("(j n) o -> j (n o)", j=4))
+        nc.gpsimd.memset(gain_rows[:], 0.0)
         make_identity(nc, ident[:])
+        nc.gpsimd.dma_start(out=vs_cols[:], in_=value_scale.rearrange("o (p t) -> (o p) t", t=PACK))
+        nc.gpsimd.dma_start(out=gain_rows[0:4, :], in_=gain.rearrange("(c n) o -> c (n o)", c=4))
+        nc.gpsimd.dma_start(out=sharp_col[:], in_=sharp)
+        nc.gpsimd.dma_start(out=os_cols[:], in_=slot_factor.rearrange("o (p t) -> (o p) t", t=PACK))
 
         warm = held.tile([P, 1], F32, name="warm")
         warm_in = held.tile([P, 1], F32, name="warm_in")
         nc.vector.memset(warm_in[:], 0.0)
         nc.scalar.activation(out=warm[:], in_=warm_in[:], func=ACT.Tanh)
 
-        key_scales = held.tile([P, I], U8, name="key_scales", align_bytes=64)
+        vs_bank = psum.tile([P, PACK, P], F32, name="vs_bank")
+        for t in range(PACK):
+            nc.tensor.transpose(vs_bank[:, t, :], vs_cols[:, t : t + 1].to_broadcast([P, P]), ident[:])
+
         key_words = held.tile([P, I], U16, name="key_words", align_bytes=64)
-        tab_g_words = held.tile([P, I], U16, name="tab_g_words", align_bytes=64)
+        key_scales = held.tile([P, I], U8, name="key_scales", align_bytes=64)
         nc.vector.tensor_copy(key_words[:], key_pool[:].indirect(offsets[:]))
-        nc.vector.tensor_copy(tab_g_words[:], tab_pool[:].indirect(offsets[:]))
         nc.vector.tensor_copy(key_scales[:], key_pool_scales[:].indirect(offsets[:]))
 
-        q_grouped = held.tile([P, Q, PACK], BF16, name="q_grouped", tag="slot_d", align_bytes=64)
+        q_grouped = held.tile([P, Q, PACK], BF16, name="q_grouped", align_bytes=64)
         q_codes = held.tile([P, Q], U32, name="q_codes", align_bytes=64)
         q_scales = held.tile([P, Q], U8, name="q_scales", align_bytes=64)
         interleave(nc, q_grouped[:], q_raw[:])
         quantize(nc, q_codes[:], q_scales[:], q_grouped[:])
-
         scores = psum.tile([Q, I], F32, name="scores", tag="scores")
         nc.tensor.matmul_mx(
             out=scores[:],
@@ -121,101 +124,135 @@ def tile_attend_lrgained_bygroup_kernel(
             stop=True,
         )
 
-        w_grouped = [
-            held.tile([P, HALF, PACK], BF16, name=f"w_grouped{h}", tag=f"w_grouped{h}", align_bytes=64) for h in range(2)
-        ]
-        w_scales = [held.tile([P, HALF], U8, name=f"w_scales{h}", align_bytes=64) for h in range(2)]
-        interleave(nc, w_grouped[0][:], w_raw[0][:])
+        w_grouped = [held.tile([P, P, PACK], BF16, name=f"w_grouped{c}", align_bytes=64) for c in range(3)]
+        w_grouped.append(reuse.tile([P, P, PACK], BF16, name="w_grouped3", offset=18432, align_bytes=64))
+        w_codes = [reuse.tile([P, P], U32, name=f"w_codes{c}", offset=16384 + 512 * c, align_bytes=64) for c in range(2)]
+        w_codes.extend(held.tile([P, P], U32, name=f"w_codes{c}", align_bytes=64) for c in range(2, 4))
+        w_scales = [held.tile([P, P], U8, name=f"w_scales{c}", align_bytes=64) for c in range(4)]
+        ht = [reuse.tile([P, I], F32, name=f"ht{c}", offset=(4608, 8960)[c]) for c in range(2)]
+        ht.extend(held.tile([P, I], F32, name=f"ht{c}") for c in range(2, 4))
+        pieces = [(0, 2 * P, "zh1"), (2 * P, P, "zh2"), (3 * P, P, "scores")]
+        h_grouped = [held.tile([P, n, PACK], BF16, name=f"h_grouped{r0}", align_bytes=64) for r0, n, tag in pieces]
+        h_codes = [held.tile([P, n], U32, name=f"h_codes{r0}", align_bytes=64) for r0, n, tag in pieces]
+        h_scales = [held.tile([P, n], U8, name=f"h_scales{r0}", align_bytes=64) for r0, n, tag in pieces]
+        zh = []
 
-        p = reuse.tile([Q, I], F32, name="p", offset=0)
-        nc.scalar.activation(out=p[:], in_=scores[:], func=ACT.Exp)
+        def weights_in(c):
+            interleave(nc, w_grouped[c][:], w_raw[c // 2][:, :, (c % 2) * P : (c % 2 + 1) * P])
 
-        cols_bank = psum.tile([P, 2, P], F32, name="cols_bank", tag="turn0")
-        nc.tensor.transpose(cols_bank[:, 0, :], rows[:], ident[:])
-        cols = reuse.tile([P, 16], F32, name="cols", offset=2048)
-        nc.scalar.copy(out=cols[:], in_=cols_bank[:, 0, 0:16])
-        os_row = psum.tile([P, I], F32, name="os_row")
-        vs_row = psum.tile([P, I], F32, name="vs_row")
-        for j in range(4):
-            nc.tensor.transpose(os_row[:, j * P : (j + 1) * P], cols[:, j : j + 1].to_broadcast([P, P]), ident[:])
-        for j in range(4):
-            nc.tensor.transpose(vs_row[:, j * P : (j + 1) * P], cols[:, 4 + j : 5 + j].to_broadcast([P, P]), ident[:])
+        def weights_quantize(c):
+            quantize(nc, w_codes[c][:], w_scales[c][:], w_grouped[c][:])
 
-        tab_g_scales = held.tile([P, I], U8, name="tab_g_scales", tag="slot_d", align_bytes=64)
-        nc.vector.tensor_copy(tab_g_scales[:], tab_pool_scales[:].indirect(offsets[:]))
-        w_codes = [
-            held.tile([P, HALF], U32, name="w_codes0", tag="slot_b", align_bytes=64),
-            held.tile([P, HALF], U32, name="w_codes1", align_bytes=64),
-        ]
-        quantize(nc, w_codes[0][:], w_scales[0][:], w_grouped[0][:])
-
-        interleave(nc, w_grouped[1][:], w_raw[1][:])
-
-        neg_sharp = held.tile([Q, 1], F32, name="neg_sharp")
-        nc.vector.tensor_scalar(neg_sharp[:], sharp_col[:], -1.0 / GROUP, None, ALU.mult)
-        score_sums = held.tile([Q, G], F32, name="score_sums", tag="w_grouped0", align_bytes=64)
-        nc.vector.tensor_reduce(score_sums[:], scores[:].rearrange("q (g j) -> q g j", j=GROUP), AX.X, ALU.add)
-        neg_ms = held.tile([Q, G], F32, name="neg_ms")
-        neg_max = held.tile([Q, 1], F32, name="neg_max")
-        nc.vector.tensor_scalar(neg_ms[:], score_sums[:], neg_sharp[:], None, ALU.mult, ALU.min, accum_out=neg_max[:])
-        s = held.tile([Q, G], F32, name="s", tag="w_grouped0", align_bytes=64)
-        nc.vector.tensor_reduce(s[:], p[:].rearrange("q (g j) -> q g j", j=GROUP), AX.X, ALU.add)
-        pg = reuse.tile([Q, G], F32, name="pg", offset=6144)
-        z = held.tile([Q, 1], F32, name="z")
-        nc.scalar.activation(out=pg[:], in_=neg_ms[:], func=ACT.Exp, bias=neg_max[:], scale=-1.0, accum_out=z[:])
-        inv_s = held.tile([Q, G], F32, name="inv_s")
-        nc.vector.reciprocal(inv_s[:], s[:])
-        quantize(nc, w_codes[1][:], w_scales[1][:], w_grouped[1][:])
-        p_os = held.tile([Q, I], F32, name="p_os")
-        nc.vector.tensor_tensor(p_os[:], p[:], os_row[:], ALU.mult)
-        inv_z = held.tile([Q, 1], F32, name="inv_z")
-        nc.vector.reciprocal(inv_z[:], z[:])
-
-        pieces = [(0, 2 * P, "scores"), (2 * P, P, "zh0"), (3 * P, P, "zh1")]
-        h_grouped = [held.tile([P, n, PACK], BF16, name=f"h_grouped{r0}", align_bytes=64) for r0, n, bank_tag in pieces]
-        h_codes = [held.tile([P, n], U32, name=f"h_codes{r0}", align_bytes=64) for r0, n, bank_tag in pieces]
-        h_scales = [held.tile([P, n], U8, name=f"h_scales{r0}", align_bytes=64) for r0, n, bank_tag in pieces]
-
-        def hidden(c):
-            h, cs = c // 2, slice((c % 2) * P, (c % 2 + 1) * P)
-            zh = psum.tile([P, I], F32, name=f"zh{c}", tag=f"zh{c % 2}")
+        def layer(c):
+            zh.append(psum.tile([P, I], F32, name=f"zh{c}", tag=f"zh{c}" if c < 3 else "scores"))
             nc.tensor.matmul_mx(
-                out=zh[:],
-                lhsT=w_codes[h][:, cs].bitcast(FP8X4),
-                lhsT_scale=w_scales[h][:, cs],
+                out=zh[c][:],
+                lhsT=w_codes[c][:].bitcast(FP8X4),
+                lhsT_scale=w_scales[c][:],
                 rhs=tab_g_words[:].bitcast(FP4X4),
                 rhs_scale=tab_g_scales[:],
                 start=True,
                 stop=True,
             )
-            ht = reuse.tile([P, I], F32, name=f"ht{c}", offset=4096 if c == 0 else 6144 + 2048 * c)
-            nc.scalar.activation(out=ht[:], in_=zh[:], func=ACT.Tanh)
-            hw = held.tile([P, I], BF16, name=f"hw{c}")
-            nc.vector.scalar_tensor_tensor(hw[:], ht[:], cols[:, 8 + c : 9 + c], vs_row[:], ALU.mult, ALU.mult)
-            bank = psum.tile([P, 2, P], F32, name=f"h_bank{c}", tag=f"turn{c % 2}")
-            turn_pairs(nc, bank[:], hw[:], ident[:], h_grouped[0][:, cs, :] if c < 2 else h_grouped[c - 1][:])
 
-        hidden(0)
-        sh = held.tile([Q, G], F32, name="sh")
-        nc.vector.scalar_tensor_tensor(sh[:], pg[:], inv_z[:], inv_s[:], ALU.mult, ALU.mult)
-        hidden(1)
-        wo = held.tile([Q, I], BF16, name="wo")
-        nc.vector.tensor_tensor(
-            wo[:].rearrange("q (g j) -> q g j", j=GROUP),
-            p_os[:].rearrange("q (g j) -> q g j", j=GROUP),
-            sh[:].unsqueeze(2).to_broadcast([Q, G, GROUP]),
+        def squash(c):
+            nc.scalar.activation(out=ht[c][:], in_=zh[c][:], func=ACT.Tanh)
+
+        def scale_and_turn(c):
+            hw = held.tile([P, P, PACK], BF16, name=f"hw{c}")
+            nc.vector.scalar_tensor_tensor(
+                hw[:],
+                ht[c][:].rearrange("p (n t) -> p n t", t=PACK),
+                gain_cols[:, c : c + 1],
+                vs_bank[:].rearrange("p t n -> p n t"),
+                ALU.mult,
+                ALU.mult,
+            )
+            bank = psum.tile([P, 2, P], F32, name=f"h_bank{c}", tag=f"turn{c % 2}")
+            grouped = h_grouped[0][:, c * P : (c + 1) * P, :] if c < 2 else h_grouped[c - 1][:]
+            turn_pairs(nc, bank[:], hw[:].rearrange("p n t -> p (n t)"), ident[:], grouped)
+
+        weights_in(0)
+        weights_in(1)
+
+        p = reuse.tile([Q, 2, P, 2], F32, name="p", offset=0)
+        nc.scalar.activation(out=p[:], in_=scores[:].rearrange("q (n u e) -> q u n e", u=2, e=2), func=ACT.Exp)
+        p_bank = psum.tile([P, PACK, Q], F32, name="p_bank")
+        for t in range(PACK):
+            nc.tensor.transpose(p_bank[:, t, :], p[:, t // 2, :, t % 2], ident[:])
+
+        gain_bank = psum.tile([P, P], F32, name="gain_bank", tag="turn0")
+        nc.tensor.transpose(gain_bank[:], gain_rows[:], ident[:])
+        gain_cols = reuse.tile([P, 4], F32, name="gain_cols", offset=2048)
+        nc.scalar.copy(out=gain_cols[:], in_=gain_bank[:, 0:4])
+
+        tab_g_words = held.tile([P, I], U16, name="tab_g_words", align_bytes=64)
+        tab_g_scales = held.tile([P, I], U8, name="tab_g_scales", align_bytes=64)
+        nc.vector.tensor_copy(tab_g_words[:], tab_pool[:].indirect(offsets[:]))
+        nc.vector.tensor_copy(tab_g_scales[:], tab_pool_scales[:].indirect(offsets[:]))
+        neg_sharp = held.tile([Q, 1], F32, name="neg_sharp")
+        nc.gpsimd.tensor_scalar(neg_sharp[:], sharp_col[:], -1.0 / GROUP, 0.0, ALU.mult, ALU.add)
+        weights_quantize(0)
+        weights_quantize(1)
+        layer(0)
+        layer(1)
+        weights_in(2)
+        weights_in(3)
+
+        score_sums = reuse.tile([Q, G], F32, name="score_sums", offset=12288)
+        nc.vector.tensor_reduce(score_sums[:], scores[:].rearrange("q (g j) -> q g j", j=GROUP), AX.X, ALU.add)
+        weights_quantize(2)
+        weights_quantize(3)
+        neg_ms = reuse.tile([Q, G], F32, name="neg_ms", offset=18688)
+        neg_max = held.tile([Q, 1], F32, name="neg_max")
+        nc.vector.tensor_scalar(neg_ms[:], score_sums[:], neg_sharp[:], None, ALU.mult, ALU.min, accum_out=neg_max[:])
+        layer(2)
+        layer(3)
+        squash(0)
+        pg = reuse.tile([Q, G], F32, name="pg", offset=6656)
+        z = held.tile([Q, 1], F32, name="z")
+        nc.scalar.activation(out=pg[:], in_=neg_ms[:], func=ACT.Exp, bias=neg_max[:], scale=-1.0, accum_out=z[:])
+        for c in range(1, 4):
+            squash(c)
+
+        s = reuse.tile([Q, G], F32, name="s", offset=18432)
+        nc.vector.tensor_reduce(s[:], p[:].rearrange("q u (g m) e -> q g u (m e)", m=2), AX.XY, ALU.add)
+        inv_s = held.tile([Q, G], F32, name="inv_s")
+        nc.vector.reciprocal(inv_s[:], s[:])
+        inv_z = held.tile([Q, 1], F32, name="inv_z")
+        nc.vector.reciprocal(inv_z[:], z[:])
+        sh = held.tile([Q, G, 2], F32, name="sh")
+        nc.vector.scalar_tensor_tensor(
+            sh[:],
+            pg[:].unsqueeze(2).to_broadcast([Q, G, 2]),
+            inv_z[:],
+            inv_s[:].unsqueeze(2).to_broadcast([Q, G, 2]),
+            ALU.mult,
             ALU.mult,
         )
+        sh_bank = psum.tile([P, Q], F32, name="sh_bank", tag="zh0")
+        nc.tensor.transpose(sh_bank[:], sh[:].rearrange("q g e -> q (g e)"), ident[:])
+        p_os = reuse.tile([P, PACK, Q], F32, name="p_os", offset=6912)
+        for t in range(PACK):
+            nc.scalar.activation(out=p_os[:, t, :], in_=p_bank[:, t, :], func=ACT.Copy, scale=os_cols[:, t : t + 1])
+        for c in range(4):
+            scale_and_turn(c)
+
         wo_grouped = held.tile([P, Q, PACK], BF16, name="wo_grouped", align_bytes=64)
         wo_codes = held.tile([P, Q], U32, name="wo_codes", align_bytes=64)
         wo_scales = held.tile([P, Q], U8, name="wo_scales", align_bytes=64)
-        wo_bank = psum.tile([P, 2, P], F32, name="wo_bank")
-        turn_pairs(nc, wo_bank[:], wo[:], ident[:], wo_grouped[:])
-
-        def finish(j):
-            r0, n, bank_tag = pieces[j]
+        nc.vector.tensor_tensor(
+            wo_grouped[:].rearrange("p (c n) t -> p c t n", n=4),
+            p_os[:].rearrange("p t (c n) -> p c t n", n=4),
+            sh_bank[:].rearrange("p (c n) -> p c n", n=4).unsqueeze(2).to_broadcast([P, Q // 4, PACK, 4]),
+            ALU.mult,
+        )
+        quantize(nc, wo_codes[:], wo_scales[:], wo_grouped[:])
+        for j in range(3):
             quantize(nc, h_codes[j][:], h_scales[j][:], h_grouped[j][:])
-            acc = psum.tile([Q, n], F32, name=f"acc{j}", tag=bank_tag)
+
+        for j, (r0, n, tag) in enumerate(pieces):
+            acc = psum.tile([Q, n], F32, name=f"acc{j}", tag=tag)
             nc.tensor.matmul_mx(
                 out=acc[:],
                 lhsT=wo_codes[:].bitcast(FP8X4),
@@ -226,11 +263,8 @@ def tile_attend_lrgained_bygroup_kernel(
                 stop=True,
             )
             result = held.tile([Q, n], F32, name=f"result{j}")
-            nc.scalar.copy(out=result[:], in_=acc[:])
+            if j == 2:
+                nc.vector.tensor_copy(out=result[:], in_=acc[:])
+            else:
+                nc.scalar.copy(out=result[:], in_=acc[:])
             nc.sync.dma_start(out=out[:, r0 : r0 + n], in_=result[:])
-
-        hidden(2)
-        quantize(nc, wo_codes[:], wo_scales[:], wo_grouped[:])
-        hidden(3)
-        for j in range(3):
-            finish(j)

@@ -25,11 +25,8 @@ HALF = R // 2
 
 
 def load_scale_rows(queue, plane, scales):
-    for quad in range(4):
-        queue.dma_start(
-            out=plane[32 * quad : 32 * quad + 4, :].bitcast(I32),
-            in_=scales[0, 4 * quad : 4 * quad + 4, :].bitcast(I32),
-        )
+    for row in range(4):
+        queue.dma_start(out=plane[row:P:32, :].bitcast(I32), in_=scales[0, row:16:4, :].bitcast(I32))
 
 
 def interleave(nc, grouped, raw):
@@ -79,17 +76,17 @@ def tile_attend_lrgained_bygroup_kernel(
         nc.vector.memset(tab_pool_scales[:].bitcast(I32), 0)
 
         w1_rows = w1.rearrange("(p t) r -> p t r", t=PACK)
-        nc.sync.dma_start(offsets[:], offs)
         nc.sync.dma_start(out=key_pool[:].bitcast(I32), in_=keys_words[0].bitcast(I32))
+        nc.sync.dma_start(offsets[:], offs)
         load_scale_rows(nc.sync, key_pool_scales, keys_scales)
         nc.sync.dma_start(out=q_raw[:], in_=query.rearrange("(p t) q -> p t q", t=PACK))
         nc.sync.dma_start(out=w_raw[0][:], in_=w1_rows[:, :, 0:HALF])
         load_scale_rows(nc.sync, tab_pool_scales, tab_scales)
         nc.sync.dma_start(out=tab_pool[:].bitcast(I32), in_=tab_words[0].bitcast(I32))
         nc.sync.dma_start(out=w_raw[1][:], in_=w1_rows[:, :, HALF:R])
+        nc.gpsimd.dma_start(out=vs_cols[:], in_=value_scale.rearrange("o (p t) -> (o p) t", t=PACK))
         nc.gpsimd.memset(gain_rows[:], 0.0)
         make_identity(nc, ident[:])
-        nc.gpsimd.dma_start(out=vs_cols[:], in_=value_scale.rearrange("o (p t) -> (o p) t", t=PACK))
         nc.gpsimd.dma_start(out=gain_rows[0:4, :], in_=gain.rearrange("(c n) o -> c (n o)", c=4))
         nc.gpsimd.dma_start(out=sharp_col[:], in_=sharp)
         nc.gpsimd.dma_start(out=os_cols[:], in_=slot_factor.rearrange("o (p t) -> (o p) t", t=PACK))
@@ -156,7 +153,14 @@ def tile_attend_lrgained_bygroup_kernel(
             )
 
         def squash(c):
-            nc.scalar.activation(out=ht[c][:], in_=zh[c][:], func=ACT.Tanh)
+            if c < 3:
+                nc.scalar.activation(out=ht[c][:], in_=zh[c][:], func=ACT.Tanh)
+            else:
+                nc.scalar.activation(
+                    out=ht[c][:].rearrange("p (u n e) -> p u n e", u=2, e=2),
+                    in_=zh[c][:].rearrange("p (n u e) -> p u n e", u=2, e=2),
+                    func=ACT.Tanh,
+                )
 
         def scale_and_turn(c):
             hw = held.tile([P, P, PACK], BF16, name=f"hw{c}")
@@ -171,6 +175,24 @@ def tile_attend_lrgained_bygroup_kernel(
             bank = psum.tile([P, 2, P], F32, name=f"h_bank{c}", tag=f"turn{c % 2}")
             grouped = h_grouped[0][:, c * P : (c + 1) * P, :] if c < 2 else h_grouped[c - 1][:]
             turn_pairs(nc, bank[:], hw[:].rearrange("p n t -> p (n t)"), ident[:], grouped)
+
+        def scale_and_turn_by_pairs(c):
+            bank = psum.tile([P, 2, P], F32, name=f"h_bank{c}", tag=f"turn{c % 2}")
+            for u in range(2):
+                hw = held.tile([P, P, 2], BF16, name=f"hw{c}_{u}")
+                nc.vector.scalar_tensor_tensor(
+                    hw[:],
+                    ht[c][:, u * (I // 2) : (u + 1) * (I // 2)].rearrange("p (n e) -> p n e", e=2),
+                    gain_cols[:, c : c + 1],
+                    vs_bank[:, 2 * u : 2 * u + 2, :].rearrange("p e n -> p n e"),
+                    ALU.mult,
+                    ALU.mult,
+                )
+                nc.tensor.transpose(bank[:, u, :], hw[:].rearrange("p n e -> p (n e)").bitcast(F32), ident[:])
+            nc.scalar.copy(
+                out=h_grouped[c - 1][:].rearrange("p c t -> p (c t)").bitcast(F32).rearrange("p (c u) -> p c u", u=2),
+                in_=bank[:].rearrange("p u c -> p c u"),
+            )
 
         weights_in(0)
         weights_in(1)
@@ -235,16 +257,17 @@ def tile_attend_lrgained_bygroup_kernel(
         p_os = reuse.tile([P, PACK, Q], F32, name="p_os", offset=6912)
         for t in range(PACK):
             nc.scalar.activation(out=p_os[:, t, :], in_=p_bank[:, t, :], func=ACT.Copy, scale=os_cols[:, t : t + 1])
-        for c in range(4):
+        for c in range(3):
             scale_and_turn(c)
+        scale_and_turn_by_pairs(3)
 
         wo_grouped = held.tile([P, Q, PACK], BF16, name="wo_grouped", align_bytes=64)
         wo_codes = held.tile([P, Q], U32, name="wo_codes", align_bytes=64)
         wo_scales = held.tile([P, Q], U8, name="wo_scales", align_bytes=64)
         nc.vector.tensor_tensor(
-            wo_grouped[:].rearrange("p (c n) t -> p c t n", n=4),
-            p_os[:].rearrange("p t (c n) -> p c t n", n=4),
-            sh_bank[:].rearrange("p (c n) -> p c n", n=4).unsqueeze(2).to_broadcast([P, Q // 4, PACK, 4]),
+            wo_grouped[:],
+            p_os[:].rearrange("p t q -> p q t"),
+            sh_bank[:].unsqueeze(2).to_broadcast([P, Q, PACK]),
             ALU.mult,
         )
         quantize(nc, wo_codes[:], wo_scales[:], wo_grouped[:])

@@ -21,12 +21,24 @@ AX = mybir.AxisListType
 P = 128
 PACK = 4
 GROUP = I // G
+CHUNKS = R // P
 HALF = R // 2
 
+W1_LOW = 0
+W1_HIGH = 6144
+HT0 = 4544
+GAIN_COLS = 6592
+PG = 6656
+P_OS = 6912
+HT1 = 8960
+TAB_POOL_SCALES = 12288
+SCORE_SUMS = 13312
+W1_GROUPED_LAST = 14336
 
-def load_scale_rows(queue, plane, scales):
+
+def load_scale_rows(nc, plane, scales):
     for row in range(4):
-        queue.dma_start(out=plane[row:P:32, :].bitcast(I32), in_=scales[0, row:16:4, :].bitcast(I32))
+        nc.sync.dma_start(out=plane[row:P:32, :].bitcast(I32), in_=scales[0, row:16:4, :].bitcast(I32))
 
 
 def interleave(nc, grouped, raw):
@@ -40,10 +52,19 @@ def quantize(nc, codes, scales, grouped):
     nc.vector.quantize_mx(out=codes.bitcast(FP8X4), scales=scales, in_=grouped.rearrange("p c t -> p (c t)"))
 
 
-def turn_pairs(nc, bank, values, ident, grouped):
-    words = values.bitcast(F32)
-    for u in range(2):
-        nc.tensor.transpose(bank[:, u, :], words[:, u : I // 2 : 2], ident)
+def product(nc, bank, codes, scales, moving, moving_scales):
+    nc.tensor.matmul_mx(
+        out=bank,
+        lhsT=codes.bitcast(FP8X4),
+        lhsT_scale=scales,
+        rhs=moving,
+        rhs_scale=moving_scales,
+        start=True,
+        stop=True,
+    )
+
+
+def join_pairs(nc, grouped, bank):
     nc.scalar.copy(
         out=grouped.rearrange("p c t -> p (c t)").bitcast(F32).rearrange("p (c u) -> p c u", u=2),
         in_=bank.rearrange("p u c -> p c u"),
@@ -62,12 +83,14 @@ def tile_attend_lrgained_bygroup_kernel(
         offsets = held.tile([P, I // 16], U16, name="offsets")
         key_pool = held.tile([P, T], U16, name="key_pool")
         key_pool_scales = held.tile([P, T], U8, name="key_pool_scales")
-        tab_pool = reuse.tile([P, T], U16, name="tab_pool", offset=12288)
-        tab_pool_scales = reuse.tile([P, T], U8, name="tab_pool_scales", offset=16384)
+        tab_pool = held.tile([P, T], U16, name="tab_pool")
+        tab_pool_scales = reuse.tile([P, T], U8, name="tab_pool_scales", offset=TAB_POOL_SCALES)
         gain_rows = held.tile([P, P], F32, name="gain_rows")
         ident = held.tile([P, P], F32, name="ident")
         q_raw = held.tile([P, PACK, Q], F32, name="q_raw")
-        w_raw = [reuse.tile([P, PACK, HALF], F32, name=f"w_raw{h}", offset=6144 * h) for h in range(2)]
+        w1_raw = [
+            reuse.tile([P, PACK, HALF], F32, name=f"w1_raw{h}", offset=at) for h, at in enumerate((W1_LOW, W1_HIGH))
+        ]
         sharp_col = held.tile([Q, 1], F32, name="sharp_col")
         os_cols = held.tile([P, PACK], F32, name="os_cols")
         vs_cols = held.tile([P, PACK], F32, name="vs_cols")
@@ -78,23 +101,23 @@ def tile_attend_lrgained_bygroup_kernel(
         w1_rows = w1.rearrange("(p t) r -> p t r", t=PACK)
         nc.sync.dma_start(out=key_pool[:].bitcast(I32), in_=keys_words[0].bitcast(I32))
         nc.sync.dma_start(offsets[:], offs)
-        load_scale_rows(nc.sync, key_pool_scales, keys_scales)
+        load_scale_rows(nc, key_pool_scales, keys_scales)
         nc.sync.dma_start(out=q_raw[:], in_=query.rearrange("(p t) q -> p t q", t=PACK))
-        nc.sync.dma_start(out=w_raw[0][:], in_=w1_rows[:, :, 0:HALF])
-        load_scale_rows(nc.sync, tab_pool_scales, tab_scales)
         nc.sync.dma_start(out=tab_pool[:].bitcast(I32), in_=tab_words[0].bitcast(I32))
-        nc.sync.dma_start(out=w_raw[1][:], in_=w1_rows[:, :, HALF:R])
-        nc.gpsimd.dma_start(out=vs_cols[:], in_=value_scale.rearrange("o (p t) -> (o p) t", t=PACK))
+        nc.sync.dma_start(out=w1_raw[0][:], in_=w1_rows[:, :, 0:HALF])
+        load_scale_rows(nc, tab_pool_scales, tab_scales)
+        nc.sync.dma_start(out=w1_raw[1][:], in_=w1_rows[:, :, HALF:R])
+        nc.sync.dma_start(out=os_cols[:], in_=slot_factor.rearrange("o (p t) -> (o p) t", t=PACK))
         nc.gpsimd.memset(gain_rows[:], 0.0)
         make_identity(nc, ident[:])
-        nc.gpsimd.dma_start(out=gain_rows[0:4, :], in_=gain.rearrange("(c n) o -> c (n o)", c=4))
+        nc.gpsimd.dma_start(out=gain_rows[0:CHUNKS, :], in_=gain.rearrange("(c n) o -> c (n o)", c=CHUNKS))
+        nc.gpsimd.dma_start(out=vs_cols[:], in_=value_scale.rearrange("o (p t) -> (o p) t", t=PACK))
         nc.gpsimd.dma_start(out=sharp_col[:], in_=sharp)
-        nc.gpsimd.dma_start(out=os_cols[:], in_=slot_factor.rearrange("o (p t) -> (o p) t", t=PACK))
 
-        warm = held.tile([P, 1], F32, name="warm")
-        warm_in = held.tile([P, 1], F32, name="warm_in")
-        nc.vector.memset(warm_in[:], 0.0)
-        nc.scalar.activation(out=warm[:], in_=warm_in[:], func=ACT.Tanh)
+        zero_bias = held.tile([P, 1], F32, name="zero_bias")
+        zero_col = held.tile([P, 1], F32, name="zero_col")
+        nc.vector.memset(zero_col[:], 0.0)
+        nc.scalar.activation(out=zero_bias[:], in_=zero_col[:], func=ACT.Tanh)
 
         vs_bank = psum.tile([P, PACK, P], F32, name="vs_bank")
         for t in range(PACK):
@@ -111,55 +134,44 @@ def tile_attend_lrgained_bygroup_kernel(
         interleave(nc, q_grouped[:], q_raw[:])
         quantize(nc, q_codes[:], q_scales[:], q_grouped[:])
         scores = psum.tile([Q, I], F32, name="scores", tag="scores")
-        nc.tensor.matmul_mx(
-            out=scores[:],
-            lhsT=q_codes[:].bitcast(FP8X4),
-            lhsT_scale=q_scales[:],
-            rhs=key_words[:].bitcast(FP4X4),
-            rhs_scale=key_scales[:],
-            start=True,
-            stop=True,
-        )
+        product(nc, scores[:], q_codes[:], q_scales[:], key_words[:].bitcast(FP4X4), key_scales[:])
 
-        w_grouped = [held.tile([P, P, PACK], BF16, name=f"w_grouped{c}", align_bytes=64) for c in range(3)]
-        w_grouped.append(reuse.tile([P, P, PACK], BF16, name="w_grouped3", offset=18432, align_bytes=64))
-        w_codes = [reuse.tile([P, P], U32, name=f"w_codes{c}", offset=16384 + 512 * c, align_bytes=64) for c in range(2)]
-        w_codes.extend(held.tile([P, P], U32, name=f"w_codes{c}", align_bytes=64) for c in range(2, 4))
-        w_scales = [held.tile([P, P], U8, name=f"w_scales{c}", align_bytes=64) for c in range(4)]
-        ht = [reuse.tile([P, I], F32, name=f"ht{c}", offset=(4608, 8960)[c]) for c in range(2)]
-        ht.extend(held.tile([P, I], F32, name=f"ht{c}") for c in range(2, 4))
+        last = CHUNKS - 1
+        w1_grouped = [held.tile([P, P, PACK], BF16, name=f"w1_grouped{c}", align_bytes=64) for c in range(last)]
+        w1_grouped.append(reuse.tile([P, P, PACK], BF16, name="w1_grouped3", offset=W1_GROUPED_LAST, align_bytes=64))
+        w1_codes = [
+            reuse.tile([P, P], U32, name=f"w1_codes{c}", offset=TAB_POOL_SCALES + 4 * P * c, align_bytes=64)
+            for c in range(2)
+        ]
+        w1_codes.extend(held.tile([P, P], U32, name=f"w1_codes{c}", align_bytes=64) for c in range(2, CHUNKS))
+        w1_scales = [held.tile([P, P], U8, name=f"w1_scales{c}", align_bytes=64) for c in range(CHUNKS)]
+        ht = [reuse.tile([P, I], F32, name=f"ht{c}", offset=at) for c, at in enumerate((HT0, HT1))]
+        ht.extend(held.tile([P, I], F32, name=f"ht{c}") for c in range(2, CHUNKS))
         pieces = [(0, 2 * P, "zh1"), (2 * P, P, "zh2"), (3 * P, P, "scores")]
         h_grouped = [held.tile([P, n, PACK], BF16, name=f"h_grouped{r0}", align_bytes=64) for r0, n, tag in pieces]
         h_codes = [held.tile([P, n], U32, name=f"h_codes{r0}", align_bytes=64) for r0, n, tag in pieces]
         h_scales = [held.tile([P, n], U8, name=f"h_scales{r0}", align_bytes=64) for r0, n, tag in pieces]
         zh = []
 
-        def weights_in(c):
-            interleave(nc, w_grouped[c][:], w_raw[c // 2][:, :, (c % 2) * P : (c % 2 + 1) * P])
+        def interleave_w1(c):
+            interleave(nc, w1_grouped[c][:], w1_raw[c // 2][:, :, (c % 2) * P : (c % 2 + 1) * P])
 
-        def weights_quantize(c):
-            quantize(nc, w_codes[c][:], w_scales[c][:], w_grouped[c][:])
+        def quantize_w1(c):
+            quantize(nc, w1_codes[c][:], w1_scales[c][:], w1_grouped[c][:])
 
         def layer(c):
-            zh.append(psum.tile([P, I], F32, name=f"zh{c}", tag=f"zh{c}" if c < 3 else "scores"))
-            nc.tensor.matmul_mx(
-                out=zh[c][:],
-                lhsT=w_codes[c][:].bitcast(FP8X4),
-                lhsT_scale=w_scales[c][:],
-                rhs=tab_g_words[:].bitcast(FP4X4),
-                rhs_scale=tab_g_scales[:],
-                start=True,
-                stop=True,
-            )
+            zh.append(psum.tile([P, I], F32, name=f"zh{c}", tag=f"zh{c}" if c < last else "scores"))
+            product(nc, zh[c][:], w1_codes[c][:], w1_scales[c][:], tab_listed[:].bitcast(FP4X4), tab_listed_scales[:])
 
         def squash(c):
-            if c < 3:
-                nc.scalar.activation(out=ht[c][:], in_=zh[c][:], func=ACT.Tanh)
+            if c < last:
+                nc.scalar.activation(out=ht[c][:], in_=zh[c][:], func=ACT.Tanh, bias=zero_bias[:])
             else:
                 nc.scalar.activation(
                     out=ht[c][:].rearrange("p (u n e) -> p u n e", u=2, e=2),
                     in_=zh[c][:].rearrange("p (n u e) -> p u n e", u=2, e=2),
                     func=ACT.Tanh,
+                    bias=zero_bias[:],
                 )
 
         def scale_and_turn(c):
@@ -173,72 +185,73 @@ def tile_attend_lrgained_bygroup_kernel(
                 ALU.mult,
             )
             bank = psum.tile([P, 2, P], F32, name=f"h_bank{c}", tag=f"turn{c % 2}")
-            grouped = h_grouped[0][:, c * P : (c + 1) * P, :] if c < 2 else h_grouped[c - 1][:]
-            turn_pairs(nc, bank[:], hw[:].rearrange("p n t -> p (n t)"), ident[:], grouped)
-
-        def scale_and_turn_by_pairs(c):
-            bank = psum.tile([P, 2, P], F32, name=f"h_bank{c}", tag=f"turn{c % 2}")
+            words = hw[:].rearrange("p n t -> p (n t)").bitcast(F32)
             for u in range(2):
-                hw = held.tile([P, P, 2], BF16, name=f"hw{c}_{u}")
+                nc.tensor.transpose(bank[:, u, :], words[:, u : I // 2 : 2], ident[:])
+            join_pairs(nc, h_grouped[0][:, c * P : (c + 1) * P, :] if c < 2 else h_grouped[c - 1][:], bank[:])
+
+        def scale_and_turn_last():
+            bank = psum.tile([P, 2, P], F32, name="h_bank3", tag=f"turn{last % 2}")
+            for u in range(2):
+                hw = held.tile([P, P, 2], BF16, name=f"hw3_{u}")
                 nc.vector.scalar_tensor_tensor(
                     hw[:],
-                    ht[c][:, u * (I // 2) : (u + 1) * (I // 2)].rearrange("p (n e) -> p n e", e=2),
-                    gain_cols[:, c : c + 1],
+                    ht[last][:, u * (I // 2) : (u + 1) * (I // 2)].rearrange("p (n e) -> p n e", e=2),
+                    gain_cols[:, last : last + 1],
                     vs_bank[:, 2 * u : 2 * u + 2, :].rearrange("p e n -> p n e"),
                     ALU.mult,
                     ALU.mult,
                 )
                 nc.tensor.transpose(bank[:, u, :], hw[:].rearrange("p n e -> p (n e)").bitcast(F32), ident[:])
-            nc.scalar.copy(
-                out=h_grouped[c - 1][:].rearrange("p c t -> p (c t)").bitcast(F32).rearrange("p (c u) -> p c u", u=2),
-                in_=bank[:].rearrange("p u c -> p c u"),
-            )
+            join_pairs(nc, h_grouped[last - 1][:], bank[:])
 
-        weights_in(0)
-        weights_in(1)
+        interleave_w1(0)
+        interleave_w1(1)
 
-        p = reuse.tile([Q, 2, P, 2], F32, name="p", offset=0)
+        p = reuse.tile([Q, 2, P, 2], F32, name="p", offset=W1_LOW)
         nc.scalar.activation(out=p[:], in_=scores[:].rearrange("q (n u e) -> q u n e", u=2, e=2), func=ACT.Exp)
-        p_bank = psum.tile([P, PACK, Q], F32, name="p_bank")
-        for t in range(PACK):
-            nc.tensor.transpose(p_bank[:, t, :], p[:, t // 2, :, t % 2], ident[:])
 
         gain_bank = psum.tile([P, P], F32, name="gain_bank", tag="turn0")
         nc.tensor.transpose(gain_bank[:], gain_rows[:], ident[:])
-        gain_cols = reuse.tile([P, 4], F32, name="gain_cols", offset=2048)
-        nc.scalar.copy(out=gain_cols[:], in_=gain_bank[:, 0:4])
 
-        tab_g_words = held.tile([P, I], U16, name="tab_g_words", align_bytes=64)
-        tab_g_scales = held.tile([P, I], U8, name="tab_g_scales", align_bytes=64)
-        nc.vector.tensor_copy(tab_g_words[:], tab_pool[:].indirect(offsets[:]))
-        nc.vector.tensor_copy(tab_g_scales[:], tab_pool_scales[:].indirect(offsets[:]))
+        tab_listed = held.tile([P, I], U16, name="tab_listed", align_bytes=64)
+        tab_listed_scales = held.tile([P, I], U8, name="tab_listed_scales", align_bytes=64)
+        nc.vector.tensor_copy(tab_listed[:], tab_pool[:].indirect(offsets[:]))
+        nc.vector.tensor_copy(tab_listed_scales[:], tab_pool_scales[:].indirect(offsets[:]))
         neg_sharp = held.tile([Q, 1], F32, name="neg_sharp")
         nc.gpsimd.tensor_scalar(neg_sharp[:], sharp_col[:], -1.0 / GROUP, 0.0, ALU.mult, ALU.add)
-        weights_quantize(0)
-        weights_quantize(1)
+        quantize_w1(0)
+        quantize_w1(1)
         layer(0)
         layer(1)
-        weights_in(2)
-        weights_in(3)
+        interleave_w1(2)
+        interleave_w1(3)
+        gain_cols = reuse.tile([P, CHUNKS], F32, name="gain_cols", offset=GAIN_COLS)
+        nc.scalar.copy(out=gain_cols[:], in_=gain_bank[:, 0:CHUNKS])
 
-        score_sums = reuse.tile([Q, G], F32, name="score_sums", offset=12288)
+        score_sums = reuse.tile([Q, G], F32, name="score_sums", offset=SCORE_SUMS)
         nc.vector.tensor_reduce(score_sums[:], scores[:].rearrange("q (g j) -> q g j", j=GROUP), AX.X, ALU.add)
-        weights_quantize(2)
-        weights_quantize(3)
-        neg_ms = reuse.tile([Q, G], F32, name="neg_ms", offset=18688)
+        quantize_w1(2)
+        quantize_w1(3)
+        neg_ms = reuse.tile([Q, G], F32, name="neg_ms", offset=W1_GROUPED_LAST + 4 * G)
         neg_max = held.tile([Q, 1], F32, name="neg_max")
         nc.vector.tensor_scalar(neg_ms[:], score_sums[:], neg_sharp[:], None, ALU.mult, ALU.min, accum_out=neg_max[:])
         layer(2)
         layer(3)
         squash(0)
-        pg = reuse.tile([Q, G], F32, name="pg", offset=6656)
+        pg = reuse.tile([Q, G], F32, name="pg", offset=PG)
         z = held.tile([Q, 1], F32, name="z")
         nc.scalar.activation(out=pg[:], in_=neg_ms[:], func=ACT.Exp, bias=neg_max[:], scale=-1.0, accum_out=z[:])
-        for c in range(1, 4):
-            squash(c)
+        squash(1)
+        p_bank = psum.tile([P, PACK, Q], F32, name="p_bank", tag="zh0")
+        for t in range(PACK):
+            nc.tensor.transpose(p_bank[:, t, :], p[:, t // 2, :, t % 2], ident[:])
+        squash(2)
+        squash(3)
 
-        s = reuse.tile([Q, G], F32, name="s", offset=18432)
+        s = reuse.tile([Q, G], F32, name="s", offset=W1_GROUPED_LAST)
         nc.vector.tensor_reduce(s[:], p[:].rearrange("q u (g m) e -> q g u (m e)", m=2), AX.XY, ALU.add)
+        scale_and_turn(0)
         inv_s = held.tile([Q, G], F32, name="inv_s")
         nc.vector.reciprocal(inv_s[:], s[:])
         inv_z = held.tile([Q, 1], F32, name="inv_z")
@@ -252,41 +265,34 @@ def tile_attend_lrgained_bygroup_kernel(
             ALU.mult,
             ALU.mult,
         )
-        sh_bank = psum.tile([P, Q], F32, name="sh_bank", tag="zh0")
-        nc.tensor.transpose(sh_bank[:], sh[:].rearrange("q g e -> q (g e)"), ident[:])
-        p_os = reuse.tile([P, PACK, Q], F32, name="p_os", offset=6912)
+        sh_bank = psum.tile([P, Q], F32, name="sh_bank")
+        nc.tensor.transpose(sh_bank[:], sh[:].rearrange("q g m -> q (g m)"), ident[:])
+        p_os = reuse.tile([P, PACK, Q], F32, name="p_os", offset=P_OS)
         for t in range(PACK):
             nc.scalar.activation(out=p_os[:, t, :], in_=p_bank[:, t, :], func=ACT.Copy, scale=os_cols[:, t : t + 1])
-        for c in range(3):
-            scale_and_turn(c)
-        scale_and_turn_by_pairs(3)
 
-        wo_grouped = held.tile([P, Q, PACK], BF16, name="wo_grouped", align_bytes=64)
-        wo_codes = held.tile([P, Q], U32, name="wo_codes", align_bytes=64)
-        wo_scales = held.tile([P, Q], U8, name="wo_scales", align_bytes=64)
+        for c in range(1, last):
+            scale_and_turn(c)
+        scale_and_turn_last()
+
+        wt_grouped = held.tile([P, Q, PACK], BF16, name="wt_grouped", align_bytes=64)
+        wt_codes = held.tile([P, Q], U32, name="wt_codes", align_bytes=64)
+        wt_scales = held.tile([P, Q], U8, name="wt_scales", align_bytes=64)
         nc.vector.tensor_tensor(
-            wo_grouped[:],
-            p_os[:].rearrange("p t q -> p q t"),
+            wt_grouped[:],
+            p_os[:].rearrange("n t q -> n q t"),
             sh_bank[:].unsqueeze(2).to_broadcast([P, Q, PACK]),
             ALU.mult,
         )
-        quantize(nc, wo_codes[:], wo_scales[:], wo_grouped[:])
-        for j in range(3):
+        quantize(nc, wt_codes[:], wt_scales[:], wt_grouped[:])
+        for j in range(len(pieces)):
             quantize(nc, h_codes[j][:], h_scales[j][:], h_grouped[j][:])
 
         for j, (r0, n, tag) in enumerate(pieces):
             acc = psum.tile([Q, n], F32, name=f"acc{j}", tag=tag)
-            nc.tensor.matmul_mx(
-                out=acc[:],
-                lhsT=wo_codes[:].bitcast(FP8X4),
-                lhsT_scale=wo_scales[:],
-                rhs=h_codes[j][:].bitcast(FP8X4),
-                rhs_scale=h_scales[j][:],
-                start=True,
-                stop=True,
-            )
+            product(nc, acc[:], wt_codes[:], wt_scales[:], h_codes[j][:].bitcast(FP8X4), h_scales[j][:])
             result = held.tile([Q, n], F32, name=f"result{j}")
-            if j == 2:
+            if j == len(pieces) - 1:
                 nc.vector.tensor_copy(out=result[:], in_=acc[:])
             else:
                 nc.scalar.copy(out=result[:], in_=acc[:])

from contextlib import ExitStack

import concourse.mybir as mybir
from concourse.masks import make_identity

D, K, R, T, I, Q, G = 512, 512, 512, 2048, 512, 128, 64
FLOPS = 2 * D * Q * I + 2 * K * R * I + 2 * I * Q * R

F32 = mybir.dt.float32
BF16 = mybir.dt.bfloat16
I32 = mybir.dt.int32
U32 = mybir.dt.uint32
U16 = mybir.dt.uint16
U8 = mybir.dt.uint8
FP8X4 = mybir.dt.float8_e4m3fn_x4
FP4X4 = mybir.dt.float4_e2m1fn_x4
ALU = mybir.AluOpType
ACT = mybir.ActivationFunctionType
AX = mybir.AxisListType

P = 128
PACK = 4
GROUP = I // G
CHUNKS = R // P
HALF = R // 2

W1_LOW = 0
W1_HIGH = 6144
HT0 = 4544
GAIN_COLS = 6592
PG = 6656
P_OS = 6912
HT1 = 8960
TAB_POOL_SCALES = 12288
SCORE_SUMS = 13312
W1_GROUPED_LAST = 14336


def load_scale_rows(nc, plane, scales):
    for row in range(4):
        nc.sync.dma_start(out=plane[row:P:32, :].bitcast(I32), in_=scales[0, row:16:4, :].bitcast(I32))


def interleave(nc, grouped, raw):
    nc.scalar.copy(
        out=grouped.rearrange("p (c n) t -> p c t n", n=4),
        in_=raw.rearrange("p t (c n) -> p c t n", n=4),
    )


def quantize(nc, codes, scales, grouped):
    nc.vector.quantize_mx(out=codes.bitcast(FP8X4), scales=scales, in_=grouped.rearrange("p c t -> p (c t)"))


def product(nc, bank, codes, scales, moving, moving_scales):
    nc.tensor.matmul_mx(
        out=bank,
        lhsT=codes.bitcast(FP8X4),
        lhsT_scale=scales,
        rhs=moving,
        rhs_scale=moving_scales,
        start=True,
        stop=True,
    )


def join_pairs(nc, grouped, bank):
    nc.scalar.copy(
        out=grouped.rearrange("p c t -> p (c t)").bitcast(F32).rearrange("p (c u) -> p c u", u=2),
        in_=bank.rearrange("p u c -> p c u"),
    )


def tile_attend_lrgained_bygroup_kernel(
    tc, query, keys_words, keys_scales, sharp, tab_words, tab_scales, w1, gain, slot_factor, value_scale, offs, out
):
    nc = tc.nc
    with ExitStack() as ctx:
        held = ctx.enter_context(tc.tile_pool(name="held", bufs=1))
        reuse = ctx.enter_context(tc.tile_pool(name="reuse", bufs=1))
        psum = ctx.enter_context(tc.psum_pool(name="psum", bufs=1))

        offsets = held.tile([P, I // 16], U16, name="offsets")
        key_pool = held.tile([P, T], U16, name="key_pool")
        key_pool_scales = held.tile([P, T], U8, name="key_pool_scales")
        tab_pool = held.tile([P, T], U16, name="tab_pool")
        tab_pool_scales = reuse.tile([P, T], U8, name="tab_pool_scales", offset=TAB_POOL_SCALES)
        gain_rows = held.tile([P, P], F32, name="gain_rows")
        ident = held.tile([P, P], F32, name="ident")
        q_raw = held.tile([P, PACK, Q], F32, name="q_raw")
        w1_raw = [
            reuse.tile([P, PACK, HALF], F32, name=f"w1_raw{h}", offset=at) for h, at in enumerate((W1_LOW, W1_HIGH))
        ]
        sharp_col = held.tile([Q, 1], F32, name="sharp_col")
        os_cols = held.tile([P, PACK], F32, name="os_cols")
        vs_cols = held.tile([P, PACK], F32, name="vs_cols")

        nc.vector.memset(key_pool_scales[:].bitcast(I32), 0)
        nc.vector.memset(tab_pool_scales[:].bitcast(I32), 0)

        w1_rows = w1.rearrange("(p t) r -> p t r", t=PACK)
        nc.sync.dma_start(out=key_pool[:].bitcast(I32), in_=keys_words[0].bitcast(I32))
        nc.sync.dma_start(offsets[:], offs)
        load_scale_rows(nc, key_pool_scales, keys_scales)
        nc.sync.dma_start(out=q_raw[:], in_=query.rearrange("(p t) q -> p t q", t=PACK))
        nc.sync.dma_start(out=tab_pool[:].bitcast(I32), in_=tab_words[0].bitcast(I32))
        nc.sync.dma_start(out=w1_raw[0][:], in_=w1_rows[:, :, 0:HALF])
        load_scale_rows(nc, tab_pool_scales, tab_scales)
        nc.sync.dma_start(out=w1_raw[1][:], in_=w1_rows[:, :, HALF:R])
        nc.sync.dma_start(out=os_cols[:], in_=slot_factor.rearrange("o (p t) -> (o p) t", t=PACK))
        nc.gpsimd.memset(gain_rows[:], 0.0)
        make_identity(nc, ident[:])
        nc.gpsimd.dma_start(out=gain_rows[0:CHUNKS, :], in_=gain.rearrange("(c n) o -> c (n o)", c=CHUNKS))
        nc.gpsimd.dma_start(out=vs_cols[:], in_=value_scale.rearrange("o (p t) -> (o p) t", t=PACK))
        nc.gpsimd.dma_start(out=sharp_col[:], in_=sharp)

        zero_bias = held.tile([P, 1], F32, name="zero_bias")
        zero_col = held.tile([P, 1], F32, name="zero_col")
        nc.vector.memset(zero_col[:], 0.0)
        nc.scalar.activation(out=zero_bias[:], in_=zero_col[:], func=ACT.Tanh)

        vs_bank = psum.tile([P, PACK, P], F32, name="vs_bank")
        for t in range(PACK):
            nc.tensor.transpose(vs_bank[:, t, :], vs_cols[:, t : t + 1].to_broadcast([P, P]), ident[:])

        key_words = held.tile([P, I], U16, name="key_words", align_bytes=64)
        key_scales = held.tile([P, I], U8, name="key_scales", align_bytes=64)
        nc.vector.tensor_copy(key_words[:], key_pool[:].indirect(offsets[:]))
        nc.vector.tensor_copy(key_scales[:], key_pool_scales[:].indirect(offsets[:]))

        q_grouped = held.tile([P, Q, PACK], BF16, name="q_grouped", align_bytes=64)
        q_codes = held.tile([P, Q], U32, name="q_codes", align_bytes=64)
        q_scales = held.tile([P, Q], U8, name="q_scales", align_bytes=64)
        interleave(nc, q_grouped[:], q_raw[:])
        quantize(nc, q_codes[:], q_scales[:], q_grouped[:])
        scores = psum.tile([Q, I], F32, name="scores", tag="scores")
        product(nc, scores[:], q_codes[:], q_scales[:], key_words[:].bitcast(FP4X4), key_scales[:])

        last = CHUNKS - 1
        w1_grouped = [held.tile([P, P, PACK], BF16, name=f"w1_grouped{c}", align_bytes=64) for c in range(last)]
        w1_grouped.append(reuse.tile([P, P, PACK], BF16, name="w1_grouped3", offset=W1_GROUPED_LAST, align_bytes=64))
        w1_codes = [
            reuse.tile([P, P], U32, name=f"w1_codes{c}", offset=TAB_POOL_SCALES + 4 * P * c, align_bytes=64)
            for c in range(2)
        ]
        w1_codes.extend(held.tile([P, P], U32, name=f"w1_codes{c}", align_bytes=64) for c in range(2, CHUNKS))
        w1_scales = [held.tile([P, P], U8, name=f"w1_scales{c}", align_bytes=64) for c in range(CHUNKS)]
        ht = [reuse.tile([P, I], F32, name=f"ht{c}", offset=at) for c, at in enumerate((HT0, HT1))]
        ht.extend(held.tile([P, I], F32, name=f"ht{c}") for c in range(2, CHUNKS))
        pieces = [(0, 2 * P, "zh1"), (2 * P, P, "zh2"), (3 * P, P, "scores")]
        h_grouped = [held.tile([P, n, PACK], BF16, name=f"h_grouped{r0}", align_bytes=64) for r0, n, tag in pieces]
        h_codes = [held.tile([P, n], U32, name=f"h_codes{r0}", align_bytes=64) for r0, n, tag in pieces]
        h_scales = [held.tile([P, n], U8, name=f"h_scales{r0}", align_bytes=64) for r0, n, tag in pieces]
        zh = []

        def interleave_w1(c):
            interleave(nc, w1_grouped[c][:], w1_raw[c // 2][:, :, (c % 2) * P : (c % 2 + 1) * P])

        def quantize_w1(c):
            quantize(nc, w1_codes[c][:], w1_scales[c][:], w1_grouped[c][:])

        def layer(c):
            zh.append(psum.tile([P, I], F32, name=f"zh{c}", tag=f"zh{c}" if c < last else "scores"))
            product(nc, zh[c][:], w1_codes[c][:], w1_scales[c][:], tab_listed[:].bitcast(FP4X4), tab_listed_scales[:])

        def squash(c):
            if c < last:
                nc.scalar.activation(out=ht[c][:], in_=zh[c][:], func=ACT.Tanh, bias=zero_bias[:])
            else:
                nc.scalar.activation(
                    out=ht[c][:].rearrange("p (u n e) -> p u n e", u=2, e=2),
                    in_=zh[c][:].rearrange("p (n u e) -> p u n e", u=2, e=2),
                    func=ACT.Tanh,
                    bias=zero_bias[:],
                )

        def scale_and_turn(c):
            hw = held.tile([P, P, PACK], BF16, name=f"hw{c}")
            nc.vector.scalar_tensor_tensor(
                hw[:],
                ht[c][:].rearrange("p (n t) -> p n t", t=PACK),
                gain_cols[:, c : c + 1],
                vs_bank[:].rearrange("p t n -> p n t"),
                ALU.mult,
                ALU.mult,
            )
            bank = psum.tile([P, 2, P], F32, name=f"h_bank{c}", tag=f"turn{c % 2}")
            words = hw[:].rearrange("p n t -> p (n t)").bitcast(F32)
            for u in range(2):
                nc.tensor.transpose(bank[:, u, :], words[:, u : I // 2 : 2], ident[:])
            join_pairs(nc, h_grouped[0][:, c * P : (c + 1) * P, :] if c < 2 else h_grouped[c - 1][:], bank[:])

        def scale_and_turn_last():
            bank = psum.tile([P, 2, P], F32, name="h_bank3", tag=f"turn{last % 2}")
            for u in range(2):
                hw = held.tile([P, P, 2], BF16, name=f"hw3_{u}")
                nc.vector.scalar_tensor_tensor(
                    hw[:],
                    ht[last][:, u * (I // 2) : (u + 1) * (I // 2)].rearrange("p (n e) -> p n e", e=2),
                    gain_cols[:, last : last + 1],
                    vs_bank[:, 2 * u : 2 * u + 2, :].rearrange("p e n -> p n e"),
                    ALU.mult,
                    ALU.mult,
                )
                nc.tensor.transpose(bank[:, u, :], hw[:].rearrange("p n e -> p (n e)").bitcast(F32), ident[:])
            join_pairs(nc, h_grouped[last - 1][:], bank[:])

        interleave_w1(0)
        interleave_w1(1)

        p = reuse.tile([Q, 2, P, 2], F32, name="p", offset=W1_LOW)
        nc.scalar.activation(out=p[:], in_=scores[:].rearrange("q (n u e) -> q u n e", u=2, e=2), func=ACT.Exp)

        gain_bank = psum.tile([P, P], F32, name="gain_bank", tag="turn0")
        nc.tensor.transpose(gain_bank[:], gain_rows[:], ident[:])

        tab_listed = held.tile([P, I], U16, name="tab_listed", align_bytes=64)
        tab_listed_scales = held.tile([P, I], U8, name="tab_listed_scales", align_bytes=64)
        nc.vector.tensor_copy(tab_listed[:], tab_pool[:].indirect(offsets[:]))
        nc.vector.tensor_copy(tab_listed_scales[:], tab_pool_scales[:].indirect(offsets[:]))
        neg_sharp = held.tile([Q, 1], F32, name="neg_sharp")
        nc.gpsimd.tensor_scalar(neg_sharp[:], sharp_col[:], -1.0 / GROUP, 0.0, ALU.mult, ALU.add)
        quantize_w1(0)
        quantize_w1(1)
        layer(0)
        layer(1)
        interleave_w1(2)
        interleave_w1(3)
        gain_cols = reuse.tile([P, CHUNKS], F32, name="gain_cols", offset=GAIN_COLS)
        nc.scalar.copy(out=gain_cols[:], in_=gain_bank[:, 0:CHUNKS])

        score_sums = reuse.tile([Q, G], F32, name="score_sums", offset=SCORE_SUMS)
        nc.vector.tensor_reduce(score_sums[:], scores[:].rearrange("q (g j) -> q g j", j=GROUP), AX.X, ALU.add)
        quantize_w1(2)
        quantize_w1(3)
        neg_ms = reuse.tile([Q, G], F32, name="neg_ms", offset=W1_GROUPED_LAST + 4 * G)
        neg_max = held.tile([Q, 1], F32, name="neg_max")
        nc.vector.tensor_scalar(neg_ms[:], score_sums[:], neg_sharp[:], None, ALU.mult, ALU.min, accum_out=neg_max[:])
        layer(2)
        layer(3)
        squash(0)
        pg = reuse.tile([Q, G], F32, name="pg", offset=PG)
        z = held.tile([Q, 1], F32, name="z")
        nc.scalar.activation(out=pg[:], in_=neg_ms[:], func=ACT.Exp, bias=neg_max[:], scale=-1.0, accum_out=z[:])
        squash(1)
        p_bank = psum.tile([P, PACK, Q], F32, name="p_bank", tag="zh0")
        for t in range(PACK):
            nc.tensor.transpose(p_bank[:, t, :], p[:, t // 2, :, t % 2], ident[:])
        squash(2)
        squash(3)

        s = reuse.tile([Q, G], F32, name="s", offset=W1_GROUPED_LAST)
        nc.vector.tensor_reduce(s[:], p[:].rearrange("q u (g m) e -> q g u (m e)", m=2), AX.XY, ALU.add)
        scale_and_turn(0)
        inv_s = held.tile([Q, G], F32, name="inv_s")
        nc.vector.reciprocal(inv_s[:], s[:])
        inv_z = held.tile([Q, 1], F32, name="inv_z")
        nc.vector.reciprocal(inv_z[:], z[:])
        sh = held.tile([Q, G, 2], F32, name="sh")
        nc.vector.scalar_tensor_tensor(
            sh[:],
            pg[:].unsqueeze(2).to_broadcast([Q, G, 2]),
            inv_z[:],
            inv_s[:].unsqueeze(2).to_broadcast([Q, G, 2]),
            ALU.mult,
            ALU.mult,
        )
        sh_bank = psum.tile([P, Q], F32, name="sh_bank")
        nc.tensor.transpose(sh_bank[:], sh[:].rearrange("q g m -> q (g m)"), ident[:])
        p_os = reuse.tile([P, PACK, Q], F32, name="p_os", offset=P_OS)
        for t in range(PACK):
            nc.scalar.activation(out=p_os[:, t, :], in_=p_bank[:, t, :], func=ACT.Copy, scale=os_cols[:, t : t + 1])

        for c in range(1, last):
            scale_and_turn(c)
        scale_and_turn_last()

        wt_grouped = held.tile([P, Q, PACK], BF16, name="wt_grouped", align_bytes=64)
        wt_codes = held.tile([P, Q], U32, name="wt_codes", align_bytes=64)
        wt_scales = held.tile([P, Q], U8, name="wt_scales", align_bytes=64)
        nc.vector.tensor_tensor(
            wt_grouped[:],
            p_os[:].rearrange("n t q -> n q t"),
            sh_bank[:].unsqueeze(2).to_broadcast([P, Q, PACK]),
            ALU.mult,
        )
        quantize(nc, wt_codes[:], wt_scales[:], wt_grouped[:])
        for j in range(len(pieces)):
            quantize(nc, h_codes[j][:], h_scales[j][:], h_grouped[j][:])

        for j, (r0, n, tag) in enumerate(pieces):
            acc = psum.tile([Q, n], F32, name=f"acc{j}", tag=tag)
            product(nc, acc[:], wt_codes[:], wt_scales[:], h_codes[j][:].bitcast(FP8X4), h_scales[j][:])
            result = held.tile([Q, n], F32, name=f"result{j}")
            if j == len(pieces) - 1:
                nc.vector.tensor_copy(out=result[:], in_=acc[:])
            else:
                nc.scalar.copy(out=result[:], in_=acc[:])
            nc.sync.dma_start(out=out[:, r0 : r0 + n], in_=result[:])
